import numpy as np
import ml_dtypes


def mxq(x, axis, fmt="e4m3"):
    dtype, down = {"e4m3": (ml_dtypes.float8_e4m3fn, 7), "e5m2": (ml_dtypes.float8_e5m2, 14)}[fmt]
    v = np.moveaxis(np.asarray(x, np.float32).astype(ml_dtypes.bfloat16).astype(np.float64), axis, -1)
    blocks = v.reshape(v.shape[:-1] + (-1, 32))
    amax = np.abs(blocks).max(-1, keepdims=True)
    byte = np.maximum(np.where(amax > 0, np.frexp(amax)[1] - 1 + 127, 0) - down, 1)
    scale = np.exp2(byte - 127.0)
    codes = (blocks / scale).astype(np.float32).astype(dtype).astype(np.float64)
    return np.moveaxis((codes * scale).reshape(v.shape), -1, axis)


WIDE = False


def mx_kscale(k):
    if not WIDE:
        return np.ones(k)
    levels = np.array([10, -10, 5, -5, 0])
    if k % 512:
        return np.exp2(np.random.permutation(np.resize(levels, k // 32))).repeat(32)
    a = np.empty((k // 512, 16))
    for p in range(k // 512):
        a[p, :8] = np.random.permutation(np.resize(levels, 8))
        for g in range(8):
            far = levels[np.abs(levels - a[p, g]) >= 10]
            a[p, g + 8] = far[np.random.randint(len(far))]
    return np.exp2(a.ravel()).repeat(32)


def f64(x):
    return np.asarray(x).astype(np.float64)


def striped(idx):
    return np.tile(idx.reshape(-1, 16).T, (8, 1)).astype(np.uint16)


def unstriped(offs):
    return offs[:16].T.reshape(-1).astype(np.int64)


def pack_weight(w):
    k, n = w.shape
    w = f64(np.asarray(w, np.float32).astype(ml_dtypes.bfloat16)).reshape(k // 32, 32, n)
    amax = np.abs(w).max(1)
    byte = np.clip(np.where(amax > 0, np.frexp(amax)[1] - 1 + 127 - 7, 1), 1, 254)
    scaled = (w * np.exp2(127.0 - byte)[:, None, :]).reshape(k, n).astype(np.float32)
    words = np.ascontiguousarray(scaled.reshape(k // 512, 128, 4, n).transpose(0, 1, 3, 2)).astype(ml_dtypes.float8_e4m3fn).view(np.uint8)
    return words, np.ascontiguousarray(byte.astype(np.uint8).reshape(k // 512, 16, n))


def unpack_weight(words, scales):
    g, p, n, _ = words.shape
    vals = np.ascontiguousarray(words).view(ml_dtypes.float8_e4m3fn).astype(np.float64) * np.repeat(np.exp2(scales.astype(np.float64) - 127.0), 8, axis=1)[..., None]
    return vals.transpose(0, 1, 3, 2).reshape(g * 512, n)


K, T, D, S, V, N = 512, 1024, 4, 1024, 256, 128


def setup_inputs():
    n = np.random.standard_normal
    s = mx_kscale(K)[:, None]
    packed = pack_weight(n((K, T)) * s)
    return {
        "x_words": packed[0],
        "x_scales": packed[1],
        "w": (n((D, K, N)) / np.sqrt(D * K) / s[None]).astype(np.float32),
        "b": (0.3 * n((N, 1))).astype(np.float32),
        "gate": np.tile(np.random.uniform(0.2, 1.0, S), (N, 1)).astype(np.float32),
        "offs": striped(np.random.permutation(T)[:S]),
    }


def reference(x_words, x_scales, w, b, gate, offs):
    idx = unstriped(offs)
    xq = unpack_weight(x_words, x_scales)[:, idx]
    wq = mxq(f64(w), 1, "e4m3")
    y = sum(wq[d].T @ xq[:, d * V:(d + 1) * V] for d in range(D))
    y = y + f64(b)
    out = np.zeros((N, T))
    out[:, idx] = f64(gate) * np.tile(y, (1, D))
    return out

from contextlib import ExitStack

import concourse.mybir as mybir

K, T, D, V, M = 512, 1024, 4, 256, 128
FLOPS = 2 * D * K * V * M

F32 = mybir.dt.float32
BF16 = mybir.dt.bfloat16
I32 = mybir.dt.int32
U32 = mybir.dt.uint32
U16 = mybir.dt.uint16
U8 = mybir.dt.uint8
FP8X4 = mybir.dt.float8_e4m3fn_x4
COPY = mybir.ActivationFunctionType.Copy
IDENTITY = mybir.ActivationFunctionType.Identity
MULT = mybir.AluOpType.mult

P = 128
PACK = 4
H = V // 2


def tile_picked_tome_lin_bias_sub_p_kernel(tc, x_words, x_scales, w, b, gate, offs, out):
    nc = tc.nc
    with ExitStack() as ctx:
        keep = ctx.enter_context(tc.tile_pool(name="keep", bufs=1))
        shared = ctx.enter_context(tc.tile_pool(name="shared", bufs=1))
        psum = ctx.enter_context(tc.psum_pool(name="psum", bufs=1))

        offsets = keep.tile([P, D * V // 16], U16, name="offsets")
        nc.sync.dma_start(offsets[:], offs)

        def entries(first, last):
            return offsets[:, first // 16 : last // 16]

        x_bytes = keep.tile([P, T], U8, name="x_bytes", align_bytes=64)
        nc.vector.memset(x_bytes[:].bitcast(I32), 0)
        for q in range(4):
            nc.scalar.dma_start(x_bytes[32 * q : 32 * q + 4, :].bitcast(I32), x_scales[0, 4 * q : 4 * q + 4, :].bitcast(I32))

        x_tile = keep.tile([P, T], I32, name="x_tile", align_bytes=64)
        w_raw = [keep.tile([P, PACK, M], F32, name=f"w_raw{d}") for d in range(D - 1)]
        w_raw.append(shared.tile([P, PACK, M], F32, name="w_raw3", offset=0, align_bytes=64))

        def load_w(d):
            nc.sync.dma_start(w_raw[d][:], w[d].rearrange("(p j) m -> p j m", j=PACK))

        load_w(0)
        nc.sync.dma_start(x_tile[:], x_words[0].rearrange("p c r -> p (c r)").bitcast(I32))
        for d in range(1, D):
            load_w(d)
        bias = keep.tile([P, 1], F32, name="bias")
        nc.sync.dma_start(bias[:], b)
        gates = keep.tile([P, D * V], F32, name="gates")
        nc.sync.dma_start(gates[:], gate)

        x_u32 = x_tile[:].bitcast(U32)
        words = {}
        scale_bytes = {}

        def gather_bytes(dst, first, last):
            nc.vector.tensor_copy(dst, x_bytes[:].indirect(entries(first, last)))
            for i, s in enumerate(range(first, last, H)):
                scale_bytes[s] = dst[:, i * H : (i + 1) * H]

        def gather_words(dst, first, last):
            nc.vector.tensor_copy(dst, x_u32.indirect(entries(first, last)))
            for i, s in enumerate(range(first, last, H)):
                words[s] = dst[:, i * H : (i + 1) * H]

        early = [(0, 640), (768, 896)]
        late = [(640, 768), (896, 1024)]
        for first, last in early:
            g = keep.tile([P, last - first], U8, name=f"gb{first}", align_bytes=64)
            gather_bytes(g[:], first, last)
        for first, last in early:
            g = keep.tile([P, last - first], U32, name=f"gw{first}", align_bytes=64)
            gather_words(g[:], first, last)

        w_codes = []
        w_scales = []
        for d in range(D):
            w_bf = keep.tile([P, M, PACK], BF16, name=f"w_bf{d}", align_bytes=64)
            nc.scalar.activation(w_bf[:], w_raw[d][:].rearrange("p j m -> p m j"), COPY)
            codes = keep.tile([P, M], U32, name=f"w_codes{d}", align_bytes=64)
            scales = keep.tile([P, M], U8, name=f"w_scales{d}", align_bytes=64)
            nc.vector.quantize_mx(out=codes[:].bitcast(FP8X4), scales=scales[:], in_=w_bf[:].rearrange("p m j -> p (m j)"))
            w_codes.append(codes)
            w_scales.append(scales)

        place = 0
        for first, last in late:
            g = shared.tile([P, H], U32, name=f"gw{first}", align_bytes=64, offset=place)
            gather_words(g[:], first, last)
            place = place + 4 * H
            g = shared.tile([P, H], U8, name=f"gb{first}", align_bytes=64, offset=place)
            gather_bytes(g[:], first, last)
            place = place + H

        acc = [psum.tile([P, H], F32, name=f"acc{h}") for h in range(2)]
        for h in range(2):
            for d in range(D):
                s = d * V + h * H
                nc.tensor.matmul_mx(
                    out=acc[h][:],
                    lhsT=w_codes[d][:].bitcast(FP8X4),
                    lhsT_scale=w_scales[d][:],
                    rhs=words[s].bitcast(FP8X4),
                    rhs_scale=scale_bytes[s],
                    start=(d == 0),
                    stop=(d == D - 1),
                )

        window = keep.tile([P, T], F32, name="window")
        cuts = [(0, H), (H, 2 * V), (2 * V, 4 * V)]
        y = [keep.tile([P, last - first], F32, name=f"y{first}") for first, last in cuts]
        nc.scalar.activation(y[0][:], acc[0][:], IDENTITY, bias=bias[:])
        nc.scalar.activation(y[1][:, H : 2 * H], acc[0][:], IDENTITY, bias=bias[:])
        y1 = y[1][:].rearrange("p (a v) -> p a v", v=H)
        y2 = y[2][:].rearrange("p (a h v) -> p h a v", h=2, v=H)
        nc.scalar.activation(y1[:, 0:3:2, :], acc[1][:].unsqueeze(1).to_broadcast([P, 2, H]), IDENTITY, bias=bias[:])
        for h in range(2):
            nc.scalar.activation(y2[:, h, :, :], acc[h][:].unsqueeze(1).to_broadcast([P, 2, H]), IDENTITY, bias=bias[:])
        for i, (first, last) in enumerate(cuts):
            nc.vector.tensor_tensor(window[:].indirect(entries(first, last)), y[i][:], gates[:, first:last], MULT)
        nc.sync.dma_start(out, window[:])
